import numpy as np
import ml_dtypes


def mxq(x, axis, fmt="e4m3"):
    dtype, down = {"e4m3": (ml_dtypes.float8_e4m3fn, 7), "e5m2": (ml_dtypes.float8_e5m2, 14)}[fmt]
    v = np.moveaxis(np.asarray(x, np.float32).astype(ml_dtypes.bfloat16).astype(np.float64), axis, -1)
    blocks = v.reshape(v.shape[:-1] + (-1, 32))
    amax = np.abs(blocks).max(-1, keepdims=True)
    byte = np.maximum(np.where(amax > 0, np.frexp(amax)[1] - 1 + 127, 0) - down, 1)
    scale = np.exp2(byte - 127.0)
    codes = (blocks / scale).astype(np.float32).astype(dtype).astype(np.float64)
    return np.moveaxis((codes * scale).reshape(v.shape), -1, axis)


WIDE = False


def mx_kscale(k):
    if not WIDE:
        return np.ones(k)
    levels = np.array([10, -10, 5, -5, 0])
    if k % 512:
        return np.exp2(np.random.permutation(np.resize(levels, k // 32))).repeat(32)
    a = np.empty((k // 512, 16))
    for p in range(k // 512):
        a[p, :8] = np.random.permutation(np.resize(levels, 8))
        for g in range(8):
            far = levels[np.abs(levels - a[p, g]) >= 10]
            a[p, g + 8] = far[np.random.randint(len(far))]
    return np.exp2(a.ravel()).repeat(32)


BF16 = ml_dtypes.bfloat16


def bf(x):
    return np.asarray(x, np.float32).astype(BF16)


def f64(x):
    return np.asarray(x).astype(np.float64)


E2M1 = np.array([0.0, 0.5, 1.0, 1.5, 2.0, 3.0, 4.0, 6.0, -0.0, -0.5, -1.0, -1.5, -2.0, -3.0, -4.0, -6.0])


def pack_weight(w, fmt):
    k, n = w.shape
    w = f64(bf(w)).reshape(k // 32, 32, n)
    amax = np.abs(w).max(1)
    if fmt == "e4m3":
        byte = np.frexp(amax)[1] - 1 + 127 - 7
    else:
        mant, ex = np.frexp(amax / 6.0)
        byte = np.where(mant > 0.5, ex, ex - 1) + 127
    byte = np.clip(np.where(amax > 0, byte, 1), 1, 254)
    scaled = (w * np.exp2(127.0 - byte)[:, None, :]).reshape(k, n).astype(np.float32)
    by_word = np.ascontiguousarray(scaled.reshape(k // 512, 128, 4, n).transpose(0, 1, 3, 2))
    if fmt == "e4m3":
        words = by_word.astype(ml_dtypes.float8_e4m3fn).view(np.uint8)
    else:
        c = by_word.astype(ml_dtypes.float4_e2m1fn).view(np.uint8) & 0xF
        words = c[..., 0::2] | (c[..., 1::2] << 4)
    return np.ascontiguousarray(words), np.ascontiguousarray(byte.astype(np.uint8).reshape(k // 512, 16, n))


def unpack_weight(words, scales, fmt):
    g, p, n, _ = words.shape
    if fmt == "e4m3":
        vals = np.ascontiguousarray(words).view(ml_dtypes.float8_e4m3fn).astype(np.float64)
    else:
        nib = np.empty((g, p, n, 4), np.uint8)
        nib[..., 0::2] = words & 0xF
        nib[..., 1::2] = words >> 4
        vals = E2M1[nib]
    vals = vals * np.repeat(np.exp2(scales.astype(np.float64) - 127.0), 8, axis=1)[..., None]
    return vals.transpose(0, 1, 3, 2).reshape(g * 512, n)


N, DA, C, F, DB, K = 1024, 512, 512, 1024, 128, 4
J = 3 * K * DB


def sigmoid(v):
    return 1.0 / (1.0 + np.exp(-v))


def softmax(v, axis):
    e = np.exp(v - v.max(axis=axis, keepdims=True))
    return e / e.sum(axis=axis, keepdims=True)


def draw0():
    sa, sc = mx_kscale(DA), mx_kscale(C)
    t = mx_kscale(F)
    xa = bf(np.random.standard_normal((N, DA)) * sa)
    xb = bf(np.random.standard_normal((N, DB)))
    c = bf(np.random.standard_normal((N, C)) * sc)
    wa_words, wa_scales = pack_weight(np.random.standard_normal((DA, F)) / np.sqrt(DA) / sa[:, None] * t, "e4m3")
    wc_words, wc_scales = pack_weight(np.random.standard_normal((C, F)) / np.sqrt(C) / sc[:, None] * t, "e4m3")
    b = bf(0.3 * np.random.standard_normal(F) * t)
    wo_words, wo_scales = pack_weight(np.random.standard_normal((F, J)) / np.sqrt(F) / t[:, None], "e4m3")
    return {
        "xa": xa,
        "xb": xb,
        "c": c,
        "wa_words": wa_words,
        "wa_scales": wa_scales,
        "wc_words": wc_words,
        "wc_scales": wc_scales,
        "b": b,
        "wo_words": wo_words,
        "wo_scales": wo_scales,
    }


def conditioner(xa, c, wa_words, wa_scales, wc_words, wc_scales, b, wo_words, wo_scales):
    a = (mxq(f64(xa), 1, "e4m3") @ unpack_weight(wa_words, wa_scales, "e4m3")) + (mxq(f64(c), 1, "e4m3") @ unpack_weight(wc_words, wc_scales, "e4m3")) + f64(b)[None, :]
    h = np.maximum(a, 0.2 * a)
    return mxq(h, 1, "e4m3") @ unpack_weight(wo_words, wo_scales, "e4m3")


def core(xa, xb, c, wa_words, wa_scales, wc_words, wc_scales, b, wo_words, wo_scales):
    n, db = xb.shape
    groups = wo_words.shape[2] // (K * db)
    p = conditioner(xa, c, wa_words, wa_scales, wc_words, wc_scales, b, wo_words, wo_scales)
    p = np.reshape(p, (n, groups, K, db))
    pl = p[:, 0]
    mu = p[:, 1]
    l = p[:, 2]
    pi = softmax(pl, 1)
    z = (f64(xb)[:, None, :] - mu) * np.exp(-np.tanh(l))
    cdf = np.sum(pi * sigmoid(z), axis=1)
    u = 0.01 + 0.98 * cdf
    return np.log(u) - np.log(1.0 - u)


def e4m3fn_bytes(y):
    return np.clip(np.asarray(y, np.float64), -448.0, 448.0).astype(np.float32).astype(ml_dtypes.float8_e4m3fn).view(np.uint8)


def e4m3fn_values(b):
    return np.asarray(b, np.uint8).view(ml_dtypes.float8_e4m3fn).astype(np.float64)


def setup_inputs():
    d = draw0()
    x0 = np.asarray(d['xa']).astype(np.float64)
    s = (np.max(np.abs(x0), axis=(0,), keepdims=True) / 448.0).astype(np.float32)
    out = {}
    for k, v in d.items():
        if k == 'xa':
            out['xa_bytes'] = e4m3fn_bytes(x0 / s.astype(np.float64))
            out['xa_scale'] = s
        else:
            out[k] = v
    return out


def reference(xa_bytes, xa_scale, xb, c, wa_words, wa_scales, wc_words, wc_scales, b, wo_words, wo_scales):
    return core(e4m3fn_values(xa_bytes) * xa_scale.astype(np.float64), xb, c, wa_words, wa_scales, wc_words, wc_scales, b, wo_words, wo_scales)

@@ -1,0 +1,448 @@
+from contextlib import ExitStack
+
+import concourse.mybir as mybir
+from concourse.masks import make_identity
+
+N, DA, C, F, DB, K = 1024, 512, 512, 1024, 128, 4
+J = 3 * K * DB
+FLOPS = 2 * N * (DA + C) * F + 2 * N * F * J
+
+F32 = mybir.dt.float32
+BF16 = mybir.dt.bfloat16
+I32 = mybir.dt.int32
+U32 = mybir.dt.uint32
+U8 = mybir.dt.uint8
+FP8 = mybir.dt.float8_e4m3fn
+FP8X4 = mybir.dt.float8_e4m3fn_x4
+ACT = mybir.ActivationFunctionType
+ALU = mybir.AluOpType
+AXIS = mybir.AxisListType
+
+P = 128
+PACK = 4
+K_PASS = P * PACK
+TILES = N // P
+CHUNK_TILES = 2
+CHUNK = CHUNK_TILES * P
+CHUNKS = N // CHUNK
+PASSES = F // K_PASS
+UNITS = CHUNKS * PASSES
+BANK = 512
+SLOPE = 0.2
+SQUEEZE = 0.98
+DEFERRED = 1
+
+
+def tile_conditionalmixturelogisticcdfcouplingmap_w8_kernel(
+    tc, xa_bytes, xa_scale, xb, c, wa_words, wa_scales, wc_words, wc_scales, b, wo_words, wo_scales, out
+):
+    nc = tc.nc
+    with ExitStack() as ctx:
+        keep = ctx.enter_context(tc.tile_pool(name="keep", bufs=1))
+        work = ctx.enter_context(tc.tile_pool(name="work", bufs=4))
+        psum = ctx.enter_context(tc.psum_pool(name="psum", bufs=8))
+        ctx.enter_context(tc.manual_schedule())
+
+        def kept(name, shape, dtype):
+            return keep.tile(shape, dtype, name=name, tag=name, align_bytes=64)
+
+        def scratch(name, shape, dtype):
+            return work.tile(shape, dtype, name=name, tag=name, align_bytes=64)
+
+        def bank(dtype=F32, width=BANK):
+            return psum.tile([P, width], dtype, name="bank", tag="bank")
+
+        xa_rows = xa_bytes.rearrange("(p j) k -> p j k", j=TILES)
+        c_rows = c.rearrange("(p j) k -> p j k", j=TILES)
+        w_in = (wa_words, wc_words)
+        w_scales_in = (wa_scales, wc_scales)
+
+        xs_col = kept("xs_col", [P, PACK], F32)
+        xa_lo = kept("xa_lo", [P, 4, DA], U8)
+        xa_hi = kept("xa_hi", [P, 4, DA], U8)
+        c_parts = [kept("c_0", [P, 2, C], BF16), kept("c_1", [P, 2, C], BF16), kept("c_23", [P, 4, C], BF16)]
+        w_raw = [[kept("w_raw_%d_%d" % (s, g), [P, K_PASS], U32) for g in range(PASSES)] for s in range(2)]
+        ws_raw = [kept("ws_raw_%d" % s, [P, F], U8) for s in range(2)]
+        wo_codes = [kept("wo_codes_%d" % g, [P, J], U32) for g in range(PASSES)]
+        wo_planes = kept("wo_planes", [P, PASSES, J], U8)
+        b_col = kept("b_col", [P, PASSES, PACK], BF16)
+        xb_rows = kept("xb_rows", [P, TILES, DB], BF16)
+        ident_f = kept("ident_f", [P, P], F32)
+        ident_b = kept("ident_b", [P, P], BF16)
+
+        make_identity(nc, ident_f[:])
+        make_identity(nc, ident_b[:])
+        for s in range(2):
+            nc.vector.memset(ws_raw[s][:].bitcast(I32), 0)
+        nc.vector.memset(wo_planes[:].rearrange("p g n -> p (g n)").bitcast(I32), 0)
+
+        def load_words(s, g):
+            words = w_in[s][0].rearrange("p n t -> p (n t)")[:, g * K_PASS * PACK : (g + 1) * K_PASS * PACK]
+            nc.sync.dma_start(out=w_raw[s][g][:].bitcast(I32), in_=words.bitcast(I32))
+
+        def load_scales(s):
+            for q in range(4):
+                nc.sync.dma_start(
+                    out=ws_raw[s][32 * q : 32 * q + 4, :].bitcast(I32),
+                    in_=w_scales_in[s][0, 4 * q : 4 * q + 4, :].bitcast(I32),
+                )
+
+        def load_wo(g):
+            nc.sync.dma_start(
+                out=wo_codes[g][:].bitcast(I32), in_=wo_words[g].rearrange("p n t -> p (n t)").bitcast(I32)
+            )
+
+        def load_wo_scales():
+            for q in range(4):
+                nc.sync.dma_start(
+                    out=wo_planes[32 * q : 32 * q + 4, :, :].bitcast(I32),
+                    in_=wo_scales[:, 4 * q : 4 * q + 4, :].rearrange("g r n -> r g n").bitcast(I32),
+                )
+
+        nc.sync.dma_start(out=xs_col[:], in_=xa_scale.rearrange("o (p t) -> p (o t)", t=PACK))
+        nc.sync.dma_start(out=xa_lo[:], in_=xa_rows[:, 0:4, :])
+        load_scales(0)
+        nc.sync.dma_start(out=c_parts[0][:], in_=c_rows[:, 0:2, :])
+        load_words(0, 0)
+        load_words(1, 0)
+        load_scales(1)
+        nc.sync.dma_start(out=c_parts[1][:], in_=c_rows[:, 2:4, :])
+        nc.sync.dma_start(out=b_col[:], in_=b.rearrange("(g p t) -> p g t", g=PASSES, t=PACK))
+        load_words(0, 1)
+        load_words(1, 1)
+        nc.sync.dma_start(out=xa_hi[:], in_=xa_rows[:, 4:8, :])
+        nc.sync.dma_start(out=xb_rows[:], in_=xb.rearrange("(p j) d -> p j d", j=TILES))
+        load_wo_scales()
+        load_wo(0)
+        load_wo(1)
+        nc.sync.dma_start(out=c_parts[2][:], in_=c_rows[:, 4:8, :])
+
+        def c_tile(j):
+            return c_parts[j // 2][:, j % 2, :] if j < 4 else c_parts[2][:, j - 4, :]
+
+        def xa_tile(j):
+            return xa_lo[:, j, :] if j < 4 else xa_hi[:, j - 4, :]
+
+        xs_row = kept("xs_row", [P, DA], F32)
+        xa_wide = [kept("xa_wide_%d" % j, [P, DA], BF16) for j in range(TILES)]
+        w_codes = [[kept("w_codes_%d_%d" % (s, g), [P, K_PASS], U32) for g in range(PASSES)] for s in range(2)]
+        w_planes = [kept("w_planes_%d" % s, [P, F], U8) for s in range(2)]
+        xb_t = kept("xb_t", [P, N], BF16)
+        x_grouped = [kept("x_grouped_%d" % ch, [P, 2 * CHUNK * PACK], BF16) for ch in range(CHUNKS)]
+        x_codes = [kept("x_codes_%d" % ch, [P, 2 * CHUNK], U32) for ch in range(CHUNKS)]
+        x_planes = [kept("x_planes_%d" % ch, [P, 2 * CHUNK], U8) for ch in range(CHUNKS)]
+        h_codes = [kept("h_codes_%d" % u, [P, CHUNK], U32) for u in range(UNITS)]
+        h_planes = [kept("h_planes_%d" % u, [P, CHUNK], U8) for u in range(UNITS)]
+        ends = kept("ends", [P, TILES, 2, DB], F32)
+        live = {}
+
+        def spread_scale():
+            bk = bank()
+            for t in range(PACK):
+                nc.tensor.transpose(bk[:, t * P : (t + 1) * P], xs_col[:, t : t + 1].to_broadcast([P, P]), ident_f[:])
+            nc.scalar.copy(
+                out=xs_row[:].rearrange("p (u m e) -> p u m e", u=2, e=2),
+                in_=bk[:].rearrange("p (u e m) -> p u m e", u=2, e=2),
+            )
+
+        def widen(j):
+            nc.vector.tensor_tensor(
+                out=xa_wide[j][:].rearrange("p (u m e) -> p u m e", u=2, e=2),
+                in0=xa_tile(j).bitcast(FP8).rearrange("p (m u e) -> p u m e", u=2, e=2),
+                in1=xs_row[:].rearrange("p (u m e) -> p u m e", u=2, e=2),
+                op=ALU.mult,
+            )
+
+        def permute_words(s, g, copy, dtype):
+            copy(
+                out=w_codes[s][g][:].bitcast(dtype).rearrange("p (t m) -> p m t", t=PACK),
+                in_=w_raw[s][g][:].bitcast(dtype).rearrange("p (m t) -> p m t", t=PACK),
+            )
+
+        def permute_scales(s):
+            nc.vector.tensor_copy(
+                out=w_planes[s][:].rearrange("p (g t m) -> p g t m", g=PASSES, t=PACK),
+                in_=ws_raw[s][:].rearrange("p (g m t) -> p g t m", g=PASSES, t=PACK),
+            )
+
+        def turn(s, ch):
+            bk = bank()
+            for jj in range(CHUNK_TILES):
+                j = ch * CHUNK_TILES + jj
+                for u in range(2):
+                    if s == 0:
+                        words = xa_wide[j][:].bitcast(F32)[:, u * P : (u + 1) * P]
+                    else:
+                        words = c_tile(j).bitcast(F32)[:, u::2]
+                    nc.tensor.transpose(bk[:, (2 * jj + u) * P : (2 * jj + u + 1) * P], words, ident_f[:])
+            live["turn", s, ch] = bk
+
+        def group_x(s, ch):
+            words = x_grouped[ch][:].bitcast(F32)[:, s * BANK : (s + 1) * BANK]
+            nc.scalar.copy(
+                out=words.rearrange("p (j r u) -> p j r u", j=CHUNK_TILES, u=2),
+                in_=live["turn", s, ch][:].rearrange("p (j u r) -> p j r u", j=CHUNK_TILES, u=2),
+            )
+
+        def quantize_x(ch):
+            nc.vector.quantize_mx(out=x_codes[ch][:].bitcast(FP8X4), scales=x_planes[ch][:], in_=x_grouped[ch][:])
+
+        def turn_xb():
+            bk = bank(BF16, N)
+            for j in range(TILES):
+                nc.tensor.transpose(bk[:, j * P : (j + 1) * P], xb_rows[:, j, :], ident_b[:])
+            live["xb"] = bk
+
+        def hidden_matmuls(u):
+            ch, g = divmod(u, PASSES)
+            banks = [bank(), bank()]
+            for t in range(PACK):
+                cols = slice(t * P, (t + 1) * P)
+                for s in range(2):
+                    tok = slice(s * CHUNK, (s + 1) * CHUNK)
+                    nc.tensor.matmul_mx(
+                        out=banks[t // 2][:, (t % 2) * CHUNK : (t % 2 + 1) * CHUNK],
+                        lhsT=w_codes[s][g][:, cols].bitcast(FP8X4),
+                        lhsT_scale=w_planes[s][:, g * K_PASS + t * P : g * K_PASS + (t + 1) * P],
+                        rhs=x_codes[ch][:, tok].bitcast(FP8X4),
+                        rhs_scale=x_planes[ch][:, tok],
+                        start=(s == 0),
+                        stop=(s == 1),
+                    )
+            live["a", u] = [banks[t // 2][:, (t % 2) * CHUNK : (t % 2 + 1) * CHUNK] for t in range(PACK)]
+
+        def add_bias(u, ts=range(PACK)):
+            g = u % PASSES
+            if ("pre", u) not in live:
+                live["pre", u] = scratch("pre", [P, PACK, CHUNK], F32)
+            for t in ts:
+                nc.scalar.activation(
+                    out=live["pre", u][:, t, :], in_=live["a", u][t], func=ACT.Identity, bias=b_col[:, g, t : t + 1], scale=1.0
+                )
+
+        def leaky(u):
+            grouped = scratch("h_grouped", [P, CHUNK * PACK], BF16)
+            pre = live["pre", u][:].rearrange("p t n -> p n t")
+            nc.vector.scalar_tensor_tensor(
+                out=grouped[:].rearrange("p (n t) -> p n t", t=PACK), in0=pre, scalar=SLOPE, in1=pre, op0=ALU.mult, op1=ALU.max
+            )
+            live["h_grouped", u] = grouped
+
+        def group_h(u, copy, lo, hi):
+            copy(
+                out=live["h_grouped", u][:, lo * PACK : hi * PACK].rearrange("p (c i t) -> p c t i", i=4, t=PACK),
+                in_=live["h_rows", u][:, :, lo:hi].rearrange("p t (c i) -> p c t i", i=4),
+            )
+
+        def quantize_h(u):
+            nc.vector.quantize_mx(
+                out=h_codes[u][:].bitcast(FP8X4), scales=h_planes[u][:], in_=live["h_grouped", u][:]
+            )
+
+        def mixture_matmuls(i):
+            ch, jj = divmod(i, CHUNK_TILES)
+            tok = slice(jj * P, (jj + 1) * P)
+            for name, grp in (("l", 2), ("mu", 1), ("pl", 0)):
+                bk = bank()
+                for k in range(K):
+                    cols = slice((grp * K + k) * DB, (grp * K + k + 1) * DB)
+                    for g in range(PASSES):
+                        u = ch * PASSES + g
+                        nc.tensor.matmul_mx(
+                            out=bk[:, k * P : (k + 1) * P],
+                            lhsT=wo_codes[g][:, cols].bitcast(FP8X4),
+                            lhsT_scale=wo_planes[:, g, cols],
+                            rhs=h_codes[u][:, tok].bitcast(FP8X4),
+                            rhs_scale=h_planes[u][:, tok],
+                            start=(g == 0),
+                            stop=(g == PASSES - 1),
+                        )
+                live[name, i] = bk
+
+        def by_k(ap):
+            return ap.rearrange("p (k n) -> p k n", k=K)
+
+        def over_k(ap):
+            return ap.unsqueeze(1).to_broadcast([P, K, P])
+
+        def logit_max(i):
+            top = scratch("top", [P, P], F32)
+            nc.vector.tensor_reduce(
+                out=top[:], in_=live["pl", i][:].rearrange("p (k n) -> p n k", k=K), axis=AXIS.X, op=ALU.max
+            )
+            live["top", i] = top
+
+        def logit_shift(i):
+            shifted = scratch("shifted", [P, BANK], F32)
+            nc.vector.tensor_tensor(
+                out=by_k(shifted[:]), in0=by_k(live["pl", i][:]), in1=over_k(live["top", i][:]), op=ALU.subtract
+            )
+            live["shifted", i] = shifted
+
+        def act(name, src, i, func, scale):
+            dst = scratch(name, [P, BANK], F32)
+            nc.scalar.activation(out=dst[:], in_=live[src, i][:], func=func, scale=scale)
+            live[name, i] = dst
+
+        def offset(i):
+            diff = scratch("diff", [P, BANK], F32)
+            nc.vector.tensor_tensor(
+                out=by_k(diff[:]), in0=over_k(xb_t[:, i * P : (i + 1) * P]), in1=by_k(live["mu", i][:]), op=ALU.subtract
+            )
+            live["diff", i] = diff
+
+        def standardize(i):
+            z = scratch("z", [P, BANK], F32)
+            nc.vector.tensor_tensor(out=z[:], in0=live["diff", i][:], in1=live["inv_scale", i][:], op=ALU.mult)
+            live["z", i] = z
+
+        def weigh(i):
+            upper = scratch("upper", [P, BANK], F32)
+            nc.vector.scalar_tensor_tensor(
+                out=upper[:],
+                in0=live["tanh_z", i][:],
+                scalar=1.0 / SQUEEZE,
+                in1=live["weight", i][:],
+                op0=ALU.add,
+                op1=ALU.mult,
+            )
+            live["upper", i] = upper
+
+        def sum_components(i):
+            bk = bank()
+            for half, name in enumerate(("weight", "upper")):
+                for k in range(K):
+                    nc.tensor.matmul(
+                        out=bk[:, half * P : (half + 1) * P],
+                        lhsT=live[name, i][:, k * P : (k + 1) * P],
+                        rhs=ident_f[:],
+                        is_transpose=True,
+                        start=(k == 0),
+                        stop=(k == K - 1),
+                    )
+            live["sums", i] = bk
+
+        def keep_upper(i, copy):
+            copy(out=ends[:, i, 0, :], in_=live["sums", i][:, P : 2 * P])
+
+        def lower(i):
+            nc.vector.scalar_tensor_tensor(
+                out=ends[:, i, 1, :],
+                in0=live["sums", i][:, 0:P],
+                scalar=2.0 / SQUEEZE,
+                in1=ends[:, i, 0, :],
+                op0=ALU.mult,
+                op1=ALU.subtract,
+            )
+
+        out_rows = out.rearrange("(p j) d -> p j d", j=TILES)
+
+        def logs(lo, hi):
+            lg = kept("logs_%d" % lo, [P, hi - lo, 2, DB], F32)
+            nc.scalar.activation(out=lg[:], in_=ends[:, lo:hi, :, :], func=ACT.Ln)
+            live["logs", lo] = lg
+
+        def finish(lo, hi):
+            lg = live["logs", lo]
+            res = kept("res_%d" % lo, [P, hi - lo, DB], F32)
+            nc.vector.tensor_tensor(out=res[:], in0=lg[:, :, 0, :], in1=lg[:, :, 1, :], op=ALU.subtract)
+            nc.sync.dma_start(out=out_rows[:, lo:hi, :], in_=res[:])
+
+        spread_scale()
+        turn(1, 0)
+        group_x(1, 0)
+        permute_scales(0)
+        widen(0)
+        widen(1)
+        permute_words(0, 0, nc.scalar.copy, U32)
+        turn(0, 0)
+        group_x(0, 0)
+        permute_words(1, 0, nc.scalar.copy, U32)
+        widen(2)
+        widen(3)
+        turn(0, 1)
+        turn(1, 1)
+        permute_scales(1)
+        quantize_x(0)
+        hidden_matmuls(0)
+        group_x(0, 1)
+        group_x(1, 1)
+        permute_words(0, 1, nc.vector.tensor_copy, I32)
+        permute_words(1, 1, nc.vector.tensor_copy, I32)
+        hidden_matmuls(1)
+        add_bias(0)
+        widen(4)
+        quantize_x(1)
+        hidden_matmuls(2)
+        widen(5)
+        leaky(0)
+        add_bias(1)
+        quantize_h(0)
+        turn_xb()
+        leaky(1)
+        add_bias(2)
+        nc.scalar.copy(out=xb_t[:], in_=live["xb"][:])
+        widen(6)
+        quantize_h(1)
+        mixture_matmuls(0)
+        widen(7)
+        leaky(2)
+        turn(0, 2)
+        turn(1, 2)
+
+        act("tanh_l", "l", 0, ACT.Tanh, 1.0)
+        for i in range(TILES):
+            u = i + 3
+            hidden = u < UNITS
+            finishing = i < TILES - DEFERRED
+            if hidden:
+                hidden_matmuls(u)
+            if i >= 2 and i - 1 < TILES - DEFERRED:
+                keep_upper(i - 2, nc.scalar.copy)
+            if i in (0, 2):
+                group_x(0, i // 2 + 2)
+            act("inv_scale", "tanh_l", i, ACT.Exp, -1.0)
+            offset(i)
+            logit_max(i)
+            if i >= 2 and i - 1 < TILES - DEFERRED:
+                lower(i - 2)
+            if u - 1 < UNITS:
+                quantize_h(u - 1)
+            logit_shift(i)
+            if i + 1 < TILES:
+                mixture_matmuls(i + 1)
+            if i in (0, 2):
+                group_x(1, i // 2 + 2)
+            if hidden:
+                add_bias(u)
+            standardize(i)
+            if i >= 1 and finishing:
+                weigh(i - 1)
+            act("weight", "shifted", i, ACT.Exp, 1.0)
+            act("tanh_z", "z", i, ACT.Tanh, 0.5)
+            if i >= 1 and finishing:
+                sum_components(i - 1)
+            if i == 1:
+                turn(0, 3)
+                turn(1, 3)
+            if i in (0, 2):
+                quantize_x(i // 2 + 2)
+            if hidden:
+                leaky(u)
+            if i + 1 < TILES:
+                act("tanh_l", "l", i + 1, ACT.Tanh, 1.0)
+
+        first = TILES - DEFERRED - 1
+        for i in range(first, TILES):
+            weigh(i)
+            sum_components(i)
+        logs(0, 3)
+        logs(3, first)
+        for i in range(first, TILES):
+            keep_upper(i, nc.vector.tensor_copy)
+        finish(0, 3)
+        for i in range(first, TILES):
+            lower(i)
+        logs(first, TILES)
+        finish(3, first)
+        finish(first, TILES)

@@ -214,25 +214,27 @@ def tile_conditionalmixturelogisticcdfcouplingmap_w8_kernel(
         def add_bias(u, ts=range(PACK)):
             g = u % PASSES
             if ("pre", u) not in live:
-                live["pre", u] = scratch("pre", [P, PACK, CHUNK], F32)
+                live["pre", u] = scratch("pre", [P, 2, 2, CHUNK], F32)
             for t in ts:
                 nc.scalar.activation(
-                    out=live["pre", u][:, t, :], in_=live["a", u][t], func=ACT.Identity, bias=b_col[:, g, t : t + 1], scale=1.0
+                    out=live["pre", u][:, t % 2, t // 2, :], in_=live["a", u][t], func=ACT.Identity, bias=b_col[:, g, t : t + 1], scale=1.0
                 )
 
         def leaky(u):
-            grouped = scratch("h_grouped", [P, CHUNK * PACK], BF16)
-            pre = live["pre", u][:].rearrange("p t n -> p n t")
+            pairs = scratch("h_pairs", [P, CHUNK * PACK], BF16)
+            pre = live["pre", u][:].rearrange("p e v n -> p (v n) e")
             nc.vector.scalar_tensor_tensor(
-                out=grouped[:].rearrange("p (n t) -> p n t", t=PACK), in0=pre, scalar=SLOPE, in1=pre, op0=ALU.mult, op1=ALU.max
+                out=pairs[:].rearrange("p (w e) -> p w e", e=2), in0=pre, scalar=SLOPE, in1=pre, op0=ALU.mult, op1=ALU.max
+            )
+            live["h_pairs", u] = pairs
+
+        def group_h(u):
+            grouped = scratch("h_grouped", [P, CHUNK * PACK], BF16)
+            nc.scalar.copy(
+                out=grouped[:].bitcast(F32).rearrange("p (n v) -> p n v", v=2),
+                in_=live["h_pairs", u][:].bitcast(F32).rearrange("p (v n) -> p n v", v=2),
             )
             live["h_grouped", u] = grouped
-
-        def group_h(u, copy, lo, hi):
-            copy(
-                out=live["h_grouped", u][:, lo * PACK : hi * PACK].rearrange("p (c i t) -> p c t i", i=4, t=PACK),
-                in_=live["h_rows", u][:, :, lo:hi].rearrange("p t (c i) -> p c t i", i=4),
-            )
 
         def quantize_h(u):
             nc.vector.quantize_mx(
@@ -374,17 +376,20 @@ def tile_conditionalmixturelogisticcdfcouplingmap_w8_kernel(
         widen(4)
         quantize_x(1)
         hidden_matmuls(2)
+        turn_xb()
         widen(5)
         leaky(0)
         add_bias(1)
-        quantize_h(0)
-        turn_xb()
+        group_h(0)
         leaky(1)
-        add_bias(2)
-        nc.scalar.copy(out=xb_t[:], in_=live["xb"][:])
+        add_bias(2, range(2))
+        group_h(1)
+        quantize_h(0)
         widen(6)
         quantize_h(1)
         mixture_matmuls(0)
+        add_bias(2, range(2, PACK))
+        nc.scalar.copy(out=xb_t[:], in_=live["xb"][:])
         widen(7)
         leaky(2)
         turn(0, 2)
@@ -397,6 +402,8 @@ def tile_conditionalmixturelogisticcdfcouplingmap_w8_kernel(
             finishing = i < TILES - DEFERRED
             if hidden:
                 hidden_matmuls(u)
+            if u - 1 < UNITS:
+                group_h(u - 1)
             if i >= 2 and i - 1 < TILES - DEFERRED:
                 keep_upper(i - 2, nc.scalar.copy)
             if i in (0, 2):
@@ -404,8 +411,6 @@ def tile_conditionalmixturelogisticcdfcouplingmap_w8_kernel(
             act("inv_scale", "tanh_l", i, ACT.Exp, -1.0)
             offset(i)
             logit_max(i)
-            if i >= 2 and i - 1 < TILES - DEFERRED:
-                lower(i - 2)
             if u - 1 < UNITS:
                 quantize_h(u - 1)
             logit_shift(i)
@@ -418,6 +423,8 @@ def tile_conditionalmixturelogisticcdfcouplingmap_w8_kernel(
             standardize(i)
             if i >= 1 and finishing:
                 weigh(i - 1)
+            if i >= 2 and i - 1 < TILES - DEFERRED:
+                lower(i - 2)
             act("weight", "shifted", i, ACT.Exp, 1.0)
             act("tanh_z", "z", i, ACT.Tanh, 0.5)
             if i >= 1 and finishing:

@@ -28,9 +28,11 @@ CHUNKS = N // CHUNK
 PASSES = F // K_PASS
 UNITS = CHUNKS * PASSES
 BANK = 512
+BANKS = 8
 SLOPE = 0.2
 SQUEEZE = 0.98
-DEFERRED = 1
+AHEAD = 4
+EARLY = 4
 
 
 def tile_conditionalmixturelogisticcdfcouplingmap_w8_kernel(
@@ -40,7 +42,7 @@ def tile_conditionalmixturelogisticcdfcouplingmap_w8_kernel(
     with ExitStack() as ctx:
         keep = ctx.enter_context(tc.tile_pool(name="keep", bufs=1))
         work = ctx.enter_context(tc.tile_pool(name="work", bufs=4))
-        psum = ctx.enter_context(tc.psum_pool(name="psum", bufs=8))
+        psum = ctx.enter_context(tc.psum_pool(name="psum", bufs=1))
         ctx.enter_context(tc.manual_schedule())
 
         def kept(name, shape, dtype):
@@ -49,8 +51,15 @@ def tile_conditionalmixturelogisticcdfcouplingmap_w8_kernel(
         def scratch(name, shape, dtype):
             return work.tile(shape, dtype, name=name, tag=name, align_bytes=64)
 
-        def bank(dtype=F32, width=BANK):
-            return psum.tile([P, width], dtype, name="bank", tag="bank")
+        free_banks = list(range(BANKS))
+        held = {}
+
+        def bank(key, dtype=F32, width=BANK):
+            held[key] = free_banks.pop(0)
+            return psum.tile([P, width], dtype, name="bank", tag="bank_%d" % held[key])
+
+        def release(key):
+            free_banks.append(held.pop(key))
 
         xa_rows = xa_bytes.rearrange("(p j) k -> p j k", j=TILES)
         c_rows = c.rearrange("(p j) k -> p j k", j=TILES)
@@ -60,7 +69,7 @@ def tile_conditionalmixturelogisticcdfcouplingmap_w8_kernel(
         xs_col = kept("xs_col", [P, PACK], F32)
         xa_lo = kept("xa_lo", [P, 4, DA], U8)
         xa_hi = kept("xa_hi", [P, 4, DA], U8)
-        c_parts = [kept("c_0", [P, 2, C], BF16), kept("c_1", [P, 2, C], BF16), kept("c_23", [P, 4, C], BF16)]
+        c_parts = [kept("c_%d" % ch, [P, CHUNK_TILES, C], BF16) for ch in range(CHUNKS)]
         w_raw = [[kept("w_raw_%d_%d" % (s, g), [P, K_PASS], U32) for g in range(PASSES)] for s in range(2)]
         ws_raw = [kept("ws_raw_%d" % s, [P, F], U8) for s in range(2)]
         wo_codes = [kept("wo_codes_%d" % g, [P, J], U32) for g in range(PASSES)]
@@ -101,9 +110,9 @@ def tile_conditionalmixturelogisticcdfcouplingmap_w8_kernel(
 
         nc.sync.dma_start(out=xs_col[:], in_=xa_scale.rearrange("o (p t) -> p (o t)", t=PACK))
         nc.sync.dma_start(out=xa_lo[:], in_=xa_rows[:, 0:4, :])
-        load_scales(0)
         nc.sync.dma_start(out=c_parts[0][:], in_=c_rows[:, 0:2, :])
         load_words(0, 0)
+        load_scales(0)
         load_words(1, 0)
         load_scales(1)
         nc.sync.dma_start(out=c_parts[1][:], in_=c_rows[:, 2:4, :])
@@ -111,19 +120,20 @@ def tile_conditionalmixturelogisticcdfcouplingmap_w8_kernel(
         load_words(0, 1)
         load_words(1, 1)
         nc.sync.dma_start(out=xa_hi[:], in_=xa_rows[:, 4:8, :])
+        nc.sync.dma_start(out=c_parts[2][:], in_=c_rows[:, 4:6, :])
         nc.sync.dma_start(out=xb_rows[:], in_=xb.rearrange("(p j) d -> p j d", j=TILES))
+        nc.sync.dma_start(out=c_parts[3][:], in_=c_rows[:, 6:8, :])
         load_wo_scales()
         load_wo(0)
         load_wo(1)
-        nc.sync.dma_start(out=c_parts[2][:], in_=c_rows[:, 4:8, :])
 
         def c_tile(j):
-            return c_parts[j // 2][:, j % 2, :] if j < 4 else c_parts[2][:, j - 4, :]
+            return c_parts[j // 2][:, j % 2, :]
 
         def xa_tile(j):
             return xa_lo[:, j, :] if j < 4 else xa_hi[:, j - 4, :]
 
-        xs_row = kept("xs_row", [P, DA], F32)
+        xs_row = bank("xs")
         xa_wide = [kept("xa_wide_%d" % j, [P, DA], BF16) for j in range(TILES)]
         w_codes = [[kept("w_codes_%d_%d" % (s, g), [P, K_PASS], U32) for g in range(PASSES)] for s in range(2)]
         w_planes = [kept("w_planes_%d" % s, [P, F], U8) for s in range(2)]
@@ -137,19 +147,14 @@ def tile_conditionalmixturelogisticcdfcouplingmap_w8_kernel(
         live = {}
 
         def spread_scale():
-            bk = bank()
             for t in range(PACK):
-                nc.tensor.transpose(bk[:, t * P : (t + 1) * P], xs_col[:, t : t + 1].to_broadcast([P, P]), ident_f[:])
-            nc.scalar.copy(
-                out=xs_row[:].rearrange("p (u m e) -> p u m e", u=2, e=2),
-                in_=bk[:].rearrange("p (u e m) -> p u m e", u=2, e=2),
-            )
+                nc.tensor.transpose(xs_row[:, t::PACK], xs_col[:, t : t + 1].to_broadcast([P, P]), ident_f[:])
 
         def widen(j):
             nc.vector.tensor_tensor(
-                out=xa_wide[j][:].rearrange("p (u m e) -> p u m e", u=2, e=2),
-                in0=xa_tile(j).bitcast(FP8).rearrange("p (m u e) -> p u m e", u=2, e=2),
-                in1=xs_row[:].rearrange("p (u m e) -> p u m e", u=2, e=2),
+                out=xa_wide[j][:],
+                in0=xa_tile(j).bitcast(FP8),
+                in1=xs_row[:],
                 op=ALU.mult,
             )
 
@@ -166,14 +171,12 @@ def tile_conditionalmixturelogisticcdfcouplingmap_w8_kernel(
             )
 
         def turn(s, ch):
-            bk = bank()
+            bk = bank(("turn", s, ch))
             for jj in range(CHUNK_TILES):
                 j = ch * CHUNK_TILES + jj
                 for u in range(2):
-                    if s == 0:
-                        words = xa_wide[j][:].bitcast(F32)[:, u * P : (u + 1) * P]
-                    else:
-                        words = c_tile(j).bitcast(F32)[:, u::2]
+                    rows = xa_wide[j][:] if s == 0 else c_tile(j)
+                    words = rows.bitcast(F32)[:, u::2]
                     nc.tensor.transpose(bk[:, (2 * jj + u) * P : (2 * jj + u + 1) * P], words, ident_f[:])
             live["turn", s, ch] = bk
 
@@ -183,19 +186,24 @@ def tile_conditionalmixturelogisticcdfcouplingmap_w8_kernel(
                 out=words.rearrange("p (j r u) -> p j r u", j=CHUNK_TILES, u=2),
                 in_=live["turn", s, ch][:].rearrange("p (j u r) -> p j r u", j=CHUNK_TILES, u=2),
             )
+            release(("turn", s, ch))
 
         def quantize_x(ch):
             nc.vector.quantize_mx(out=x_codes[ch][:].bitcast(FP8X4), scales=x_planes[ch][:], in_=x_grouped[ch][:])
 
         def turn_xb():
-            bk = bank(BF16, N)
+            bk = bank("xb", BF16, N)
             for j in range(TILES):
                 nc.tensor.transpose(bk[:, j * P : (j + 1) * P], xb_rows[:, j, :], ident_b[:])
             live["xb"] = bk
 
+        def keep_xb():
+            nc.scalar.copy(out=xb_t[:], in_=live["xb"][:])
+            release("xb")
+
         def hidden_matmuls(u):
             ch, g = divmod(u, PASSES)
-            banks = [bank(), bank()]
+            banks = [bank(("a", u, 0)), bank(("a", u, 1))]
             for t in range(PACK):
                 cols = slice(t * P, (t + 1) * P)
                 for s in range(2):
@@ -219,6 +227,8 @@ def tile_conditionalmixturelogisticcdfcouplingmap_w8_kernel(
                 nc.scalar.activation(
                     out=live["pre", u][:, t % 2, t // 2, :], in_=live["a", u][t], func=ACT.Identity, bias=b_col[:, g, t : t + 1], scale=1.0
                 )
+                if t % 2 == 1:
+                    release(("a", u, t // 2))
 
         def leaky(u):
             pairs = scratch("h_pairs", [P, CHUNK * PACK], BF16)
@@ -228,9 +238,9 @@ def tile_conditionalmixturelogisticcdfcouplingmap_w8_kernel(
             )
             live["h_pairs", u] = pairs
 
-        def group_h(u):
+        def group_h(u, copy):
             grouped = scratch("h_grouped", [P, CHUNK * PACK], BF16)
-            nc.scalar.copy(
+            copy(
                 out=grouped[:].bitcast(F32).rearrange("p (n v) -> p n v", v=2),
                 in_=live["h_pairs", u][:].bitcast(F32).rearrange("p (v n) -> p n v", v=2),
             )
@@ -245,7 +255,7 @@ def tile_conditionalmixturelogisticcdfcouplingmap_w8_kernel(
             ch, jj = divmod(i, CHUNK_TILES)
             tok = slice(jj * P, (jj + 1) * P)
             for name, grp in (("l", 2), ("mu", 1), ("pl", 0)):
-                bk = bank()
+                bk = bank((name, i))
                 for k in range(K):
                     cols = slice((grp * K + k) * DB, (grp * K + k + 1) * DB)
                     for g in range(PASSES):
@@ -280,11 +290,14 @@ def tile_conditionalmixturelogisticcdfcouplingmap_w8_kernel(
                 out=by_k(shifted[:]), in0=by_k(live["pl", i][:]), in1=over_k(live["top", i][:]), op=ALU.subtract
             )
             live["shifted", i] = shifted
+            release(("pl", i))
 
         def act(name, src, i, func, scale):
             dst = scratch(name, [P, BANK], F32)
             nc.scalar.activation(out=dst[:], in_=live[src, i][:], func=func, scale=scale)
             live[name, i] = dst
+            if src == "l":
+                release(("l", i))
 
         def offset(i):
             diff = scratch("diff", [P, BANK], F32)
@@ -292,10 +305,11 @@ def tile_conditionalmixturelogisticcdfcouplingmap_w8_kernel(
                 out=by_k(diff[:]), in0=over_k(xb_t[:, i * P : (i + 1) * P]), in1=by_k(live["mu", i][:]), op=ALU.subtract
             )
             live["diff", i] = diff
+            release(("mu", i))
 
         def standardize(i):
             z = scratch("z", [P, BANK], F32)
-            nc.vector.tensor_tensor(out=z[:], in0=live["diff", i][:], in1=live["inv_scale", i][:], op=ALU.mult)
+            nc.gpsimd.tensor_tensor(out=z[:], in0=live["diff", i][:], in1=live["inv_scale", i][:], op=ALU.mult)
             live["z", i] = z
 
         def weigh(i):
@@ -310,19 +324,19 @@ def tile_conditionalmixturelogisticcdfcouplingmap_w8_kernel(
             )
             live["upper", i] = upper
 
-        def sum_components(i):
-            bk = bank()
-            for half, name in enumerate(("weight", "upper")):
-                for k in range(K):
-                    nc.tensor.matmul(
-                        out=bk[:, half * P : (half + 1) * P],
-                        lhsT=live[name, i][:, k * P : (k + 1) * P],
-                        rhs=ident_f[:],
-                        is_transpose=True,
-                        start=(k == 0),
-                        stop=(k == K - 1),
-                    )
-            live["sums", i] = bk
+        def sum_components(i, name):
+            if name == "weight":
+                live["sums", i] = bank(("sums", i))
+            half = ("weight", "upper").index(name)
+            for k in range(K):
+                nc.tensor.matmul(
+                    out=live["sums", i][:, half * P : (half + 1) * P],
+                    lhsT=live[name, i][:, k * P : (k + 1) * P],
+                    rhs=ident_f[:],
+                    is_transpose=True,
+                    start=(k == 0),
+                    stop=(k == K - 1),
+                )
 
         def keep_upper(i, copy):
             copy(out=ends[:, i, 0, :], in_=live["sums", i][:, P : 2 * P])
@@ -336,6 +350,7 @@ def tile_conditionalmixturelogisticcdfcouplingmap_w8_kernel(
                 op0=ALU.mult,
                 op1=ALU.subtract,
             )
+            release(("sums", i))
 
         out_rows = out.rearrange("(p j) d -> p j d", j=TILES)
 
@@ -353,7 +368,6 @@ def tile_conditionalmixturelogisticcdfcouplingmap_w8_kernel(
         spread_scale()
         turn(1, 0)
         group_x(1, 0)
-        permute_scales(0)
         widen(0)
         widen(1)
         permute_words(0, 0, nc.scalar.copy, U32)
@@ -364,6 +378,7 @@ def tile_conditionalmixturelogisticcdfcouplingmap_w8_kernel(
         widen(3)
         turn(0, 1)
         turn(1, 1)
+        permute_scales(0)
         permute_scales(1)
         quantize_x(0)
         hidden_matmuls(0)
@@ -373,83 +388,106 @@ def tile_conditionalmixturelogisticcdfcouplingmap_w8_kernel(
         permute_words(1, 1, nc.vector.tensor_copy, I32)
         hidden_matmuls(1)
         add_bias(0)
-        widen(4)
         quantize_x(1)
-        hidden_matmuls(2)
-        turn_xb()
+        widen(4)
         widen(5)
+        hidden_matmuls(2)
         leaky(0)
         add_bias(1)
-        group_h(0)
-        leaky(1)
-        add_bias(2, range(2))
-        group_h(1)
-        quantize_h(0)
-        widen(6)
-        quantize_h(1)
-        mixture_matmuls(0)
-        add_bias(2, range(2, PACK))
-        nc.scalar.copy(out=xb_t[:], in_=live["xb"][:])
-        widen(7)
-        leaky(2)
         turn(0, 2)
         turn(1, 2)
-
+        widen(6)
+        group_h(0, nc.vector.tensor_copy)
+        leaky(1)
+        add_bias(2)
+        hidden_matmuls(3)
+        quantize_h(0)
+        group_h(1, nc.vector.tensor_copy)
+        group_x(0, 2)
+        group_x(1, 2)
+        widen(7)
+        release("xs")
+        quantize_h(1)
+        turn_xb()
+        turn(0, 3)
+        turn(1, 3)
+        leaky(2)
+        add_bias(3)
+        mixture_matmuls(0)
+        keep_xb()
+        quantize_x(2)
+        group_h(2, nc.vector.tensor_copy)
+        group_x(0, 3)
         act("tanh_l", "l", 0, ACT.Tanh, 1.0)
+        group_x(1, 3)
+        act("inv_scale", "tanh_l", 0, ACT.Exp, -1.0)
+        hidden_matmuls(4)
+        leaky(3)
+        quantize_h(2)
+        group_h(3, nc.scalar.copy)
+
         for i in range(TILES):
-            u = i + 3
+            u = i + AHEAD
             hidden = u < UNITS
-            finishing = i < TILES - DEFERRED
-            if hidden:
-                hidden_matmuls(u)
-            if u - 1 < UNITS:
-                group_h(u - 1)
-            if i >= 2 and i - 1 < TILES - DEFERRED:
-                keep_upper(i - 2, nc.scalar.copy)
-            if i in (0, 2):
-                group_x(0, i // 2 + 2)
-            act("inv_scale", "tanh_l", i, ACT.Exp, -1.0)
-            offset(i)
-            logit_max(i)
-            if u - 1 < UNITS:
-                quantize_h(u - 1)
-            logit_shift(i)
             if i + 1 < TILES:
                 mixture_matmuls(i + 1)
-            if i in (0, 2):
-                group_x(1, i // 2 + 2)
+            if i >= 1:
+                act("tanh_z", "z", i - 1, ACT.Tanh, 0.5)
             if hidden:
                 add_bias(u)
+            offset(i)
             standardize(i)
-            if i >= 1 and finishing:
-                weigh(i - 1)
-            if i >= 2 and i - 1 < TILES - DEFERRED:
-                lower(i - 2)
-            act("weight", "shifted", i, ACT.Exp, 1.0)
-            act("tanh_z", "z", i, ACT.Tanh, 0.5)
-            if i >= 1 and finishing:
-                sum_components(i - 1)
-            if i == 1:
-                turn(0, 3)
-                turn(1, 3)
-            if i in (0, 2):
-                quantize_x(i // 2 + 2)
-            if hidden:
-                leaky(u)
+            logit_max(i)
+            if 0 <= i - 4 < EARLY:
+                lower(i - 4)
+            logit_shift(i)
+            if 0 <= i - 2:
+                sum_components(i - 2, "weight")
+            if 0 <= i - 2 < EARLY:
+                sum_components(i - 2, "upper")
+            if u + 1 < UNITS:
+                hidden_matmuls(u + 1)
             if i + 1 < TILES:
                 act("tanh_l", "l", i + 1, ACT.Tanh, 1.0)
+            if 0 <= i - 3 < EARLY:
+                keep_upper(i - 3, nc.scalar.copy)
+            if hidden:
+                act("weight", "shifted", i, ACT.Exp, 1.0)
+            if i + 1 < TILES:
+                act("inv_scale", "tanh_l", i + 1, ACT.Exp, -1.0)
+            if not hidden:
+                act("weight", "shifted", i, ACT.Exp, 1.0)
+            if u - 1 < UNITS:
+                quantize_h(u - 1)
+            if i == 0:
+                quantize_x(3)
+            if hidden:
+                leaky(u)
+            if 0 <= i - 1 < EARLY:
+                weigh(i - 1)
+            if hidden:
+                group_h(u, nc.scalar.copy)
 
-        first = TILES - DEFERRED - 1
-        for i in range(first, TILES):
-            weigh(i)
-            sum_components(i)
-        logs(0, 3)
-        logs(3, first)
-        for i in range(first, TILES):
-            keep_upper(i, nc.vector.tensor_copy)
-        finish(0, 3)
-        for i in range(first, TILES):
+        last = TILES - 1
+        act("tanh_z", "z", last, ACT.Tanh, 0.5)
+        sum_components(last - 1, "weight")
+        sum_components(last, "weight")
+        for i in range(last - 3, EARLY):
             lower(i)
-        logs(first, TILES)
-        finish(3, first)
-        finish(first, TILES)
+        logs(0, EARLY)
+        for i in range(EARLY, TILES + 2):
+            if i < TILES:
+                weigh(i)
+                sum_components(i, "upper")
+            if EARLY <= i - 1 < TILES:
+                keep_upper(i - 1, nc.vector.tensor_copy)
+            if i == 10:
+                finish(0, EARLY)
+            if i - 2 >= EARLY:
+                lower(i - 2)
+            if i - 2 == last - 2:
+                logs(EARLY, last - 2 + 1)
+        logs(last - 2 + 1, TILES)
+        finish(0, EARLY)
+        finish(EARLY, last - 2 + 1)
+        finish(last - 2 + 1, TILES)

@@ -71,9 +71,9 @@ def tile_conditionalmixturelogisticcdfcouplingmap_w8_kernel(
         xa_hi = kept("xa_hi", [P, 4, DA], U8)
         c_parts = [kept("c_%d" % ch, [P, CHUNK_TILES, C], BF16) for ch in range(CHUNKS)]
         w_raw = [[kept("w_raw_%d_%d" % (s, g), [P, K_PASS], U32) for g in range(PASSES)] for s in range(2)]
-        ws_raw = [kept("ws_raw_%d" % s, [P, F], U8) for s in range(2)]
+        ws_raw = kept("ws_raw", [P, F], U8)
         wo_codes = [kept("wo_codes_%d" % g, [P, J], U32) for g in range(PASSES)]
-        wo_planes = kept("wo_planes", [P, PASSES, J], U8)
+        wo_planes = kept("wo_planes", [P, J], U8)
         b_col = kept("b_col", [P, PASSES, PACK], BF16)
         xb_rows = kept("xb_rows", [P, TILES, DB], BF16)
         ident_f = kept("ident_f", [P, P], F32)
@@ -81,9 +81,8 @@ def tile_conditionalmixturelogisticcdfcouplingmap_w8_kernel(
 
         make_identity(nc, ident_f[:])
         make_identity(nc, ident_b[:])
-        for s in range(2):
-            nc.vector.memset(ws_raw[s][:].bitcast(I32), 0)
-        nc.vector.memset(wo_planes[:].rearrange("p g n -> p (g n)").bitcast(I32), 0)
+        nc.vector.memset(ws_raw[:].bitcast(I32), 0)
+        nc.vector.memset(wo_planes[:].bitcast(I32), 0)
 
         def load_words(s, g):
             words = w_in[s][0].rearrange("p n t -> p (n t)")[:, g * K_PASS * PACK : (g + 1) * K_PASS * PACK]
@@ -92,7 +91,7 @@ def tile_conditionalmixturelogisticcdfcouplingmap_w8_kernel(
         def load_scales(s):
             for q in range(4):
                 nc.sync.dma_start(
-                    out=ws_raw[s][32 * q : 32 * q + 4, :].bitcast(I32),
+                    out=ws_raw[32 * q + 4 * s : 32 * q + 4 * s + 4, :].bitcast(I32),
                     in_=w_scales_in[s][0, 4 * q : 4 * q + 4, :].bitcast(I32),
                 )
 
@@ -104,8 +103,8 @@ def tile_conditionalmixturelogisticcdfcouplingmap_w8_kernel(
         def load_wo_scales():
             for q in range(4):
                 nc.sync.dma_start(
-                    out=wo_planes[32 * q : 32 * q + 4, :, :].bitcast(I32),
-                    in_=wo_scales[:, 4 * q : 4 * q + 4, :].rearrange("g r n -> r g n").bitcast(I32),
+                    out=wo_planes[32 * q : 32 * q + 4 * PASSES, :].bitcast(I32),
+                    in_=wo_scales[:, 4 * q : 4 * q + 4, :].bitcast(I32),
                 )
 
         nc.sync.dma_start(out=xs_col[:], in_=xa_scale.rearrange("o (p t) -> p (o t)", t=PACK))
@@ -136,7 +135,7 @@ def tile_conditionalmixturelogisticcdfcouplingmap_w8_kernel(
         xs_row = bank("xs")
         xa_wide = [kept("xa_wide_%d" % j, [P, DA], BF16) for j in range(TILES)]
         w_codes = [[kept("w_codes_%d_%d" % (s, g), [P, K_PASS], U32) for g in range(PASSES)] for s in range(2)]
-        w_planes = [kept("w_planes_%d" % s, [P, F], U8) for s in range(2)]
+        w_planes = kept("w_planes", [P, F], U8)
         xb_t = kept("xb_t", [P, N], BF16)
         x_grouped = [kept("x_grouped_%d" % ch, [P, 2 * CHUNK * PACK], BF16) for ch in range(CHUNKS)]
         x_codes = [kept("x_codes_%d" % ch, [P, 2 * CHUNK], U32) for ch in range(CHUNKS)]
@@ -164,10 +163,10 @@ def tile_conditionalmixturelogisticcdfcouplingmap_w8_kernel(
                 in_=w_raw[s][g][:].bitcast(dtype).rearrange("p (m t) -> p m t", t=PACK),
             )
 
-        def permute_scales(s):
+        def permute_scales():
             nc.vector.tensor_copy(
-                out=w_planes[s][:].rearrange("p (g t m) -> p g t m", g=PASSES, t=PACK),
-                in_=ws_raw[s][:].rearrange("p (g m t) -> p g t m", g=PASSES, t=PACK),
+                out=w_planes[:].rearrange("p (g t m) -> p g t m", g=PASSES, t=PACK),
+                in_=ws_raw[:].rearrange("p (g m t) -> p g t m", g=PASSES, t=PACK),
             )
 
         def turn(s, ch):
@@ -211,7 +210,7 @@ def tile_conditionalmixturelogisticcdfcouplingmap_w8_kernel(
                     nc.tensor.matmul_mx(
                         out=banks[t // 2][:, (t % 2) * CHUNK : (t % 2 + 1) * CHUNK],
                         lhsT=w_codes[s][g][:, cols].bitcast(FP8X4),
-                        lhsT_scale=w_planes[s][:, g * K_PASS + t * P : g * K_PASS + (t + 1) * P],
+                        lhsT_scale=w_planes[4 * s :, g * K_PASS + t * P : g * K_PASS + (t + 1) * P],
                         rhs=x_codes[ch][:, tok].bitcast(FP8X4),
                         rhs_scale=x_planes[ch][:, tok],
                         start=(s == 0),
@@ -263,7 +262,7 @@ def tile_conditionalmixturelogisticcdfcouplingmap_w8_kernel(
                         nc.tensor.matmul_mx(
                             out=bk[:, k * P : (k + 1) * P],
                             lhsT=wo_codes[g][:, cols].bitcast(FP8X4),
-                            lhsT_scale=wo_planes[:, g, cols],
+                            lhsT_scale=wo_planes[4 * g :, cols],
                             rhs=h_codes[u][:, tok].bitcast(FP8X4),
                             rhs_scale=h_planes[u][:, tok],
                             start=(g == 0),
@@ -373,14 +372,13 @@ def tile_conditionalmixturelogisticcdfcouplingmap_w8_kernel(
         permute_words(0, 0, nc.scalar.copy, U32)
         turn(0, 0)
         group_x(0, 0)
-        permute_words(1, 0, nc.scalar.copy, U32)
         widen(2)
         widen(3)
+        permute_words(1, 0, nc.vector.tensor_copy, I32)
         turn(0, 1)
         turn(1, 1)
-        permute_scales(0)
-        permute_scales(1)
         quantize_x(0)
+        permute_scales()
         hidden_matmuls(0)
         group_x(0, 1)
         group_x(1, 1)
@@ -435,6 +433,8 @@ def tile_conditionalmixturelogisticcdfcouplingmap_w8_kernel(
                 act("tanh_z", "z", i - 1, ACT.Tanh, 0.5)
             if hidden:
                 add_bias(u)
+            if 1 <= i and u - 1 < UNITS:
+                group_h(u - 1, nc.scalar.copy)
             offset(i)
             standardize(i)
             logit_max(i)
@@ -457,16 +457,14 @@ def tile_conditionalmixturelogisticcdfcouplingmap_w8_kernel(
                 act("inv_scale", "tanh_l", i + 1, ACT.Exp, -1.0)
             if not hidden:
                 act("weight", "shifted", i, ACT.Exp, 1.0)
-            if u - 1 < UNITS:
-                quantize_h(u - 1)
             if i == 0:
                 quantize_x(3)
             if hidden:
                 leaky(u)
+            if u - 1 < UNITS:
+                quantize_h(u - 1)
             if 0 <= i - 1 < EARLY:
                 weigh(i - 1)
-            if hidden:
-                group_h(u, nc.scalar.copy)
 
         last = TILES - 1
         act("tanh_z", "z", last, ACT.Tanh, 0.5)

from contextlib import ExitStack

import concourse.mybir as mybir
from concourse.masks import make_identity

N, DA, C, F, DB, K = 1024, 512, 512, 1024, 128, 4
J = 3 * K * DB
FLOPS = 2 * N * (DA + C) * F + 2 * N * F * J

F32 = mybir.dt.float32
BF16 = mybir.dt.bfloat16
I32 = mybir.dt.int32
U32 = mybir.dt.uint32
U8 = mybir.dt.uint8
FP8 = mybir.dt.float8_e4m3fn
FP8X4 = mybir.dt.float8_e4m3fn_x4
ACT = mybir.ActivationFunctionType
ALU = mybir.AluOpType
AXIS = mybir.AxisListType

P = 128
PACK = 4
K_PASS = P * PACK
TILES = N // P
CHUNK_TILES = 2
CHUNK = CHUNK_TILES * P
CHUNKS = N // CHUNK
PASSES = F // K_PASS
UNITS = CHUNKS * PASSES
BANK = 512
BANKS = 8
SLOPE = 0.2
SQUEEZE = 0.98
AHEAD = 4
EARLY = 4


def tile_conditionalmixturelogisticcdfcouplingmap_w8_kernel(
    tc, xa_bytes, xa_scale, xb, c, wa_words, wa_scales, wc_words, wc_scales, b, wo_words, wo_scales, out
):
    nc = tc.nc
    with ExitStack() as ctx:
        keep = ctx.enter_context(tc.tile_pool(name="keep", bufs=1))
        work = ctx.enter_context(tc.tile_pool(name="work", bufs=4))
        psum = ctx.enter_context(tc.psum_pool(name="psum", bufs=1))
        ctx.enter_context(tc.manual_schedule())

        def kept(name, shape, dtype):
            return keep.tile(shape, dtype, name=name, tag=name, align_bytes=64)

        def scratch(name, shape, dtype):
            return work.tile(shape, dtype, name=name, tag=name, align_bytes=64)

        free_banks = list(range(BANKS))
        held = {}

        def bank(key, dtype=F32, width=BANK):
            held[key] = free_banks.pop(0)
            return psum.tile([P, width], dtype, name="bank", tag="bank_%d" % held[key])

        def release(key):
            free_banks.append(held.pop(key))

        xa_rows = xa_bytes.rearrange("(p j) k -> p j k", j=TILES)
        c_rows = c.rearrange("(p j) k -> p j k", j=TILES)
        w_in = (wa_words, wc_words)
        w_scales_in = (wa_scales, wc_scales)

        xs_col = kept("xs_col", [P, PACK], F32)
        xa_lo = kept("xa_lo", [P, 4, DA], U8)
        xa_hi = kept("xa_hi", [P, 4, DA], U8)
        c_parts = [kept("c_%d" % ch, [P, CHUNK_TILES, C], BF16) for ch in range(CHUNKS)]
        w_raw = [[kept("w_raw_%d_%d" % (s, g), [P, K_PASS], U32) for g in range(PASSES)] for s in range(2)]
        ws_raw = kept("ws_raw", [P, F], U8)
        wo_codes = [kept("wo_codes_%d" % g, [P, J], U32) for g in range(PASSES)]
        wo_planes = kept("wo_planes", [P, J], U8)
        b_col = kept("b_col", [P, PASSES, PACK], BF16)
        xb_rows = kept("xb_rows", [P, TILES, DB], BF16)
        ident_f = kept("ident_f", [P, P], F32)
        ident_b = kept("ident_b", [P, P], BF16)

        make_identity(nc, ident_f[:])
        make_identity(nc, ident_b[:])
        nc.vector.memset(ws_raw[:].bitcast(I32), 0)
        nc.vector.memset(wo_planes[:].bitcast(I32), 0)

        def load_words(s, g):
            words = w_in[s][0].rearrange("p n t -> p (n t)")[:, g * K_PASS * PACK : (g + 1) * K_PASS * PACK]
            nc.sync.dma_start(out=w_raw[s][g][:].bitcast(I32), in_=words.bitcast(I32))

        def load_scales(s):
            for q in range(4):
                nc.sync.dma_start(
                    out=ws_raw[32 * q + 4 * s : 32 * q + 4 * s + 4, :].bitcast(I32),
                    in_=w_scales_in[s][0, 4 * q : 4 * q + 4, :].bitcast(I32),
                )

        def load_wo(g):
            nc.sync.dma_start(
                out=wo_codes[g][:].bitcast(I32), in_=wo_words[g].rearrange("p n t -> p (n t)").bitcast(I32)
            )

        def load_wo_scales():
            for q in range(4):
                nc.sync.dma_start(
                    out=wo_planes[32 * q : 32 * q + 4 * PASSES, :].bitcast(I32),
                    in_=wo_scales[:, 4 * q : 4 * q + 4, :].bitcast(I32),
                )

        nc.sync.dma_start(out=xs_col[:], in_=xa_scale.rearrange("o (p t) -> p (o t)", t=PACK))
        nc.sync.dma_start(out=xa_lo[:], in_=xa_rows[:, 0:4, :])
        nc.sync.dma_start(out=c_parts[0][:], in_=c_rows[:, 0:2, :])
        load_words(0, 0)
        load_scales(0)
        load_words(1, 0)
        load_scales(1)
        nc.sync.dma_start(out=c_parts[1][:], in_=c_rows[:, 2:4, :])
        nc.sync.dma_start(out=b_col[:], in_=b.rearrange("(g p t) -> p g t", g=PASSES, t=PACK))
        load_words(0, 1)
        load_words(1, 1)
        nc.sync.dma_start(out=xa_hi[:], in_=xa_rows[:, 4:8, :])
        nc.sync.dma_start(out=c_parts[2][:], in_=c_rows[:, 4:6, :])
        nc.sync.dma_start(out=xb_rows[:], in_=xb.rearrange("(p j) d -> p j d", j=TILES))
        nc.sync.dma_start(out=c_parts[3][:], in_=c_rows[:, 6:8, :])
        load_wo_scales()
        load_wo(0)
        load_wo(1)

        def c_tile(j):
            return c_parts[j // 2][:, j % 2, :]

        def xa_tile(j):
            return xa_lo[:, j, :] if j < 4 else xa_hi[:, j - 4, :]

        xs_row = bank("xs")
        xa_wide = [kept("xa_wide_%d" % j, [P, DA], BF16) for j in range(TILES)]
        w_codes = [[kept("w_codes_%d_%d" % (s, g), [P, K_PASS], U32) for g in range(PASSES)] for s in range(2)]
        w_planes = kept("w_planes", [P, F], U8)
        xb_t = kept("xb_t", [P, N], BF16)
        x_grouped = [kept("x_grouped_%d" % ch, [P, 2 * CHUNK * PACK], BF16) for ch in range(CHUNKS)]
        x_codes = [kept("x_codes_%d" % ch, [P, 2 * CHUNK], U32) for ch in range(CHUNKS)]
        x_planes = [kept("x_planes_%d" % ch, [P, 2 * CHUNK], U8) for ch in range(CHUNKS)]
        h_codes = [kept("h_codes_%d" % u, [P, CHUNK], U32) for u in range(UNITS)]
        h_planes = [kept("h_planes_%d" % u, [P, CHUNK], U8) for u in range(UNITS)]
        ends = kept("ends", [P, TILES, 2, DB], F32)
        live = {}

        def spread_scale():
            for t in range(PACK):
                nc.tensor.transpose(xs_row[:, t::PACK], xs_col[:, t : t + 1].to_broadcast([P, P]), ident_f[:])

        def widen(j):
            nc.vector.tensor_tensor(
                out=xa_wide[j][:],
                in0=xa_tile(j).bitcast(FP8),
                in1=xs_row[:],
                op=ALU.mult,
            )

        def permute_words(s, g, copy, dtype):
            copy(
                out=w_codes[s][g][:].bitcast(dtype).rearrange("p (t m) -> p m t", t=PACK),
                in_=w_raw[s][g][:].bitcast(dtype).rearrange("p (m t) -> p m t", t=PACK),
            )

        def permute_scales():
            nc.vector.tensor_copy(
                out=w_planes[:].rearrange("p (g t m) -> p g t m", g=PASSES, t=PACK),
                in_=ws_raw[:].rearrange("p (g m t) -> p g t m", g=PASSES, t=PACK),
            )

        def turn(s, ch):
            bk = bank(("turn", s, ch))
            for jj in range(CHUNK_TILES):
                j = ch * CHUNK_TILES + jj
                for u in range(2):
                    rows = xa_wide[j][:] if s == 0 else c_tile(j)
                    words = rows.bitcast(F32)[:, u::2]
                    nc.tensor.transpose(bk[:, (2 * jj + u) * P : (2 * jj + u + 1) * P], words, ident_f[:])
            live["turn", s, ch] = bk

        def group_x(s, ch):
            words = x_grouped[ch][:].bitcast(F32)[:, s * BANK : (s + 1) * BANK]
            nc.scalar.copy(
                out=words.rearrange("p (j r u) -> p j r u", j=CHUNK_TILES, u=2),
                in_=live["turn", s, ch][:].rearrange("p (j u r) -> p j r u", j=CHUNK_TILES, u=2),
            )
            release(("turn", s, ch))

        def quantize_x(ch):
            nc.vector.quantize_mx(out=x_codes[ch][:].bitcast(FP8X4), scales=x_planes[ch][:], in_=x_grouped[ch][:])

        def turn_xb():
            bk = bank("xb", BF16, N)
            for j in range(TILES):
                nc.tensor.transpose(bk[:, j * P : (j + 1) * P], xb_rows[:, j, :], ident_b[:])
            live["xb"] = bk

        def keep_xb():
            nc.scalar.copy(out=xb_t[:], in_=live["xb"][:])
            release("xb")

        def hidden_matmuls(u):
            ch, g = divmod(u, PASSES)
            banks = [bank(("a", u, 0)), bank(("a", u, 1))]
            for t in range(PACK):
                cols = slice(t * P, (t + 1) * P)
                for s in range(2):
                    tok = slice(s * CHUNK, (s + 1) * CHUNK)
                    nc.tensor.matmul_mx(
                        out=banks[t // 2][:, (t % 2) * CHUNK : (t % 2 + 1) * CHUNK],
                        lhsT=w_codes[s][g][:, cols].bitcast(FP8X4),
                        lhsT_scale=w_planes[4 * s :, g * K_PASS + t * P : g * K_PASS + (t + 1) * P],
                        rhs=x_codes[ch][:, tok].bitcast(FP8X4),
                        rhs_scale=x_planes[ch][:, tok],
                        start=(s == 0),
                        stop=(s == 1),
                    )
            live["a", u] = [banks[t // 2][:, (t % 2) * CHUNK : (t % 2 + 1) * CHUNK] for t in range(PACK)]

        def add_bias(u, ts=range(PACK)):
            g = u % PASSES
            if ("pre", u) not in live:
                live["pre", u] = scratch("pre", [P, 2, 2, CHUNK], F32)
            for t in ts:
                nc.scalar.activation(
                    out=live["pre", u][:, t % 2, t // 2, :], in_=live["a", u][t], func=ACT.Identity, bias=b_col[:, g, t : t + 1], scale=1.0
                )
                if t % 2 == 1:
                    release(("a", u, t // 2))

        def leaky(u):
            pairs = scratch("h_pairs", [P, CHUNK * PACK], BF16)
            pre = live["pre", u][:].rearrange("p e v n -> p (v n) e")
            nc.vector.scalar_tensor_tensor(
                out=pairs[:].rearrange("p (w e) -> p w e", e=2), in0=pre, scalar=SLOPE, in1=pre, op0=ALU.mult, op1=ALU.max
            )
            live["h_pairs", u] = pairs

        def group_h(u, copy):
            grouped = scratch("h_grouped", [P, CHUNK * PACK], BF16)
            copy(
                out=grouped[:].bitcast(F32).rearrange("p (n v) -> p n v", v=2),
                in_=live["h_pairs", u][:].bitcast(F32).rearrange("p (v n) -> p n v", v=2),
            )
            live["h_grouped", u] = grouped

        def quantize_h(u):
            nc.vector.quantize_mx(
                out=h_codes[u][:].bitcast(FP8X4), scales=h_planes[u][:], in_=live["h_grouped", u][:]
            )

        def mixture_matmuls(i):
            ch, jj = divmod(i, CHUNK_TILES)
            tok = slice(jj * P, (jj + 1) * P)
            for name, grp in (("l", 2), ("mu", 1), ("pl", 0)):
                bk = bank((name, i))
                for k in range(K):
                    cols = slice((grp * K + k) * DB, (grp * K + k + 1) * DB)
                    for g in range(PASSES):
                        u = ch * PASSES + g
                        nc.tensor.matmul_mx(
                            out=bk[:, k * P : (k + 1) * P],
                            lhsT=wo_codes[g][:, cols].bitcast(FP8X4),
                            lhsT_scale=wo_planes[4 * g :, cols],
                            rhs=h_codes[u][:, tok].bitcast(FP8X4),
                            rhs_scale=h_planes[u][:, tok],
                            start=(g == 0),
                            stop=(g == PASSES - 1),
                        )
                live[name, i] = bk

        def by_k(ap):
            return ap.rearrange("p (k n) -> p k n", k=K)

        def over_k(ap):
            return ap.unsqueeze(1).to_broadcast([P, K, P])

        def logit_max(i):
            top = scratch("top", [P, P], F32)
            nc.vector.tensor_reduce(
                out=top[:], in_=live["pl", i][:].rearrange("p (k n) -> p n k", k=K), axis=AXIS.X, op=ALU.max
            )
            live["top", i] = top

        def logit_shift(i):
            shifted = scratch("shifted", [P, BANK], F32)
            nc.vector.tensor_tensor(
                out=by_k(shifted[:]), in0=by_k(live["pl", i][:]), in1=over_k(live["top", i][:]), op=ALU.subtract
            )
            live["shifted", i] = shifted
            release(("pl", i))

        def act(name, src, i, func, scale):
            dst = scratch(name, [P, BANK], F32)
            nc.scalar.activation(out=dst[:], in_=live[src, i][:], func=func, scale=scale)
            live[name, i] = dst
            if src == "l":
                release(("l", i))

        def offset(i):
            diff = scratch("diff", [P, BANK], F32)
            nc.vector.tensor_tensor(
                out=by_k(diff[:]), in0=over_k(xb_t[:, i * P : (i + 1) * P]), in1=by_k(live["mu", i][:]), op=ALU.subtract
            )
            live["diff", i] = diff
            release(("mu", i))

        def standardize(i):
            z = scratch("z", [P, BANK], F32)
            nc.gpsimd.tensor_tensor(out=z[:], in0=live["diff", i][:], in1=live["inv_scale", i][:], op=ALU.mult)
            live["z", i] = z

        def weigh(i):
            upper = scratch("upper", [P, BANK], F32)
            nc.vector.scalar_tensor_tensor(
                out=upper[:],
                in0=live["tanh_z", i][:],
                scalar=1.0 / SQUEEZE,
                in1=live["weight", i][:],
                op0=ALU.add,
                op1=ALU.mult,
            )
            live["upper", i] = upper

        def sum_components(i, name):
            if name == "weight":
                live["sums", i] = bank(("sums", i))
            half = ("weight", "upper").index(name)
            for k in range(K):
                nc.tensor.matmul(
                    out=live["sums", i][:, half * P : (half + 1) * P],
                    lhsT=live[name, i][:, k * P : (k + 1) * P],
                    rhs=ident_f[:],
                    is_transpose=True,
                    start=(k == 0),
                    stop=(k == K - 1),
                )

        def keep_upper(i, copy):
            copy(out=ends[:, i, 0, :], in_=live["sums", i][:, P : 2 * P])

        def lower(i):
            nc.vector.scalar_tensor_tensor(
                out=ends[:, i, 1, :],
                in0=live["sums", i][:, 0:P],
                scalar=2.0 / SQUEEZE,
                in1=ends[:, i, 0, :],
                op0=ALU.mult,
                op1=ALU.subtract,
            )
            release(("sums", i))

        out_rows = out.rearrange("(p j) d -> p j d", j=TILES)

        def logs(lo, hi):
            lg = kept("logs_%d" % lo, [P, hi - lo, 2, DB], F32)
            nc.scalar.activation(out=lg[:], in_=ends[:, lo:hi, :, :], func=ACT.Ln)
            live["logs", lo] = lg

        def finish(lo, hi):
            lg = live["logs", lo]
            res = kept("res_%d" % lo, [P, hi - lo, DB], F32)
            nc.vector.tensor_tensor(out=res[:], in0=lg[:, :, 0, :], in1=lg[:, :, 1, :], op=ALU.subtract)
            nc.sync.dma_start(out=out_rows[:, lo:hi, :], in_=res[:])

        spread_scale()
        turn(1, 0)
        group_x(1, 0)
        widen(0)
        widen(1)
        permute_words(0, 0, nc.scalar.copy, U32)
        turn(0, 0)
        group_x(0, 0)
        widen(2)
        widen(3)
        permute_words(1, 0, nc.vector.tensor_copy, I32)
        turn(0, 1)
        turn(1, 1)
        quantize_x(0)
        permute_scales()
        hidden_matmuls(0)
        group_x(0, 1)
        group_x(1, 1)
        permute_words(0, 1, nc.vector.tensor_copy, I32)
        permute_words(1, 1, nc.vector.tensor_copy, I32)
        hidden_matmuls(1)
        add_bias(0)
        quantize_x(1)
        widen(4)
        widen(5)
        hidden_matmuls(2)
        leaky(0)
        add_bias(1)
        turn(0, 2)
        turn(1, 2)
        widen(6)
        group_h(0, nc.vector.tensor_copy)
        leaky(1)
        add_bias(2)
        hidden_matmuls(3)
        quantize_h(0)
        group_h(1, nc.vector.tensor_copy)
        group_x(0, 2)
        group_x(1, 2)
        widen(7)
        release("xs")
        quantize_h(1)
        turn_xb()
        turn(0, 3)
        turn(1, 3)
        leaky(2)
        add_bias(3)
        mixture_matmuls(0)
        keep_xb()
        quantize_x(2)
        group_h(2, nc.vector.tensor_copy)
        group_x(0, 3)
        act("tanh_l", "l", 0, ACT.Tanh, 1.0)
        group_x(1, 3)
        act("inv_scale", "tanh_l", 0, ACT.Exp, -1.0)
        hidden_matmuls(4)
        leaky(3)
        quantize_h(2)
        group_h(3, nc.scalar.copy)

        for i in range(TILES):
            u = i + AHEAD
            hidden = u < UNITS
            if i + 1 < TILES:
                mixture_matmuls(i + 1)
            if i >= 1:
                act("tanh_z", "z", i - 1, ACT.Tanh, 0.5)
            if hidden:
                add_bias(u)
            if 1 <= i and u - 1 < UNITS:
                group_h(u - 1, nc.scalar.copy)
            offset(i)
            standardize(i)
            logit_max(i)
            if 0 <= i - 4 < EARLY:
                lower(i - 4)
            logit_shift(i)
            if 0 <= i - 2:
                sum_components(i - 2, "weight")
            if 0 <= i - 2 < EARLY:
                sum_components(i - 2, "upper")
            if u + 1 < UNITS:
                hidden_matmuls(u + 1)
            if i + 1 < TILES:
                act("tanh_l", "l", i + 1, ACT.Tanh, 1.0)
            if 0 <= i - 3 < EARLY:
                keep_upper(i - 3, nc.scalar.copy)
            if hidden:
                act("weight", "shifted", i, ACT.Exp, 1.0)
            if i + 1 < TILES:
                act("inv_scale", "tanh_l", i + 1, ACT.Exp, -1.0)
            if not hidden:
                act("weight", "shifted", i, ACT.Exp, 1.0)
            if i == 0:
                quantize_x(3)
            if hidden:
                leaky(u)
            if u - 1 < UNITS:
                quantize_h(u - 1)
            if 0 <= i - 1 < EARLY:
                weigh(i - 1)

        last = TILES - 1
        act("tanh_z", "z", last, ACT.Tanh, 0.5)
        sum_components(last - 1, "weight")
        sum_components(last, "weight")
        for i in range(last - 3, EARLY):
            lower(i)
        logs(0, EARLY)
        for i in range(EARLY, TILES + 2):
            if i < TILES:
                weigh(i)
                sum_components(i, "upper")
            if EARLY <= i - 1 < TILES:
                keep_upper(i - 1, nc.vector.tensor_copy)
            if i == 10:
                finish(0, EARLY)
            if i - 2 >= EARLY:
                lower(i - 2)
            if i - 2 == last - 2:
                logs(EARLY, last - 2 + 1)
        logs(last - 2 + 1, TILES)
        finish(0, EARLY)
        finish(EARLY, last - 2 + 1)
        finish(last - 2 + 1, TILES)
